import numpy as np
import ml_dtypes


def mxq(x, axis, fmt="e4m3"):
    dtype, down = {"e4m3": (ml_dtypes.float8_e4m3fn, 7), "e5m2": (ml_dtypes.float8_e5m2, 14)}[fmt]
    v = np.moveaxis(np.asarray(x, np.float32).astype(ml_dtypes.bfloat16).astype(np.float64), axis, -1)
    blocks = v.reshape(v.shape[:-1] + (-1, 32))
    amax = np.abs(blocks).max(-1, keepdims=True)
    byte = np.maximum(np.where(amax > 0, np.frexp(amax)[1] - 1 + 127, 0) - down, 1)
    scale = np.exp2(byte - 127.0)
    codes = (blocks / scale).astype(np.float32).astype(dtype).astype(np.float64)
    return np.moveaxis((codes * scale).reshape(v.shape), -1, axis)


WIDE = False


def mx_kscale(k):
    if not WIDE:
        return np.ones(k)
    levels = np.array([10, -10, 5, -5, 0])
    if k % 512:
        return np.exp2(np.random.permutation(np.resize(levels, k // 32))).repeat(32)
    a = np.empty((k // 512, 16))
    for p in range(k // 512):
        a[p, :8] = np.random.permutation(np.resize(levels, 8))
        for g in range(8):
            far = levels[np.abs(levels - a[p, g]) >= 10]
            a[p, g + 8] = far[np.random.randint(len(far))]
    return np.exp2(a.ravel()).repeat(32)


def f64(x):
    return np.asarray(x).astype(np.float64)


def striped8(idx):
    return np.asarray(idx).reshape(8, -1, 16).transpose(0, 2, 1).reshape(128, -1).astype(np.uint16)


def unstriped8(offs):
    return offs.reshape(8, 16, -1).transpose(0, 2, 1).reshape(8, -1).astype(np.int64)


def pick8(x, idx, run):
    r = np.arange(len(x))
    return x[r[:, None], idx[r % (8 * run) // run]]


E2M1 = np.array([0.0, 0.5, 1.0, 1.5, 2.0, 3.0, 4.0, 6.0, -0.0, -0.5, -1.0, -1.5, -2.0, -3.0, -4.0, -6.0])


def pack_weight(w, fmt):
    k, n = w.shape
    w = f64(np.asarray(w, np.float32).astype(ml_dtypes.bfloat16)).reshape(k // 32, 32, n)
    amax = np.abs(w).max(1)
    if fmt == "e4m3":
        byte = np.frexp(amax)[1] - 1 + 127 - 7
    else:
        mant, ex = np.frexp(amax / 6.0)
        byte = np.where(mant > 0.5, ex, ex - 1) + 127
    byte = np.clip(np.where(amax > 0, byte, 1), 1, 254)
    scaled = (w * np.exp2(127.0 - byte)[:, None, :]).reshape(k, n).astype(np.float32)
    by_word = np.ascontiguousarray(scaled.reshape(k // 512, 128, 4, n).transpose(0, 1, 3, 2))
    if fmt == "e4m3":
        words = by_word.astype(ml_dtypes.float8_e4m3fn).view(np.uint8)
    else:
        c = by_word.astype(ml_dtypes.float4_e2m1fn).view(np.uint8) & 0xF
        words = (c[..., 0::2] | (c[..., 1::2] << 4)).reshape(k // 512, 128, 2 * n)
    return np.ascontiguousarray(words), np.ascontiguousarray(byte.astype(np.uint8).reshape(k // 512, 16, n))


def unpack_weight(words, scales, fmt):
    g, _, n = scales.shape
    words = np.ascontiguousarray(words).reshape(g, 128, n, -1)
    if fmt == "e4m3":
        vals = words.view(ml_dtypes.float8_e4m3fn).astype(np.float64)
    else:
        nib = np.empty((g, 128, n, 4), np.uint8)
        nib[..., 0::2] = words & 0xF
        nib[..., 1::2] = words >> 4
        vals = E2M1[nib]
    vals = vals * np.repeat(np.exp2(scales.astype(np.float64) - 127.0), 8, axis=1)[..., None]
    return vals.transpose(0, 1, 3, 2).reshape(g * 512, n)


def sgn(shape):
    return np.random.uniform(0.5, 2.0, shape) * np.where(np.random.standard_normal(shape) < 0, -1.0, 1.0)


D, T, U, I, Q = 512, 1024, 1024, 512, 128


def setup_inputs():
    n = np.random.standard_normal
    idx = np.stack([np.random.permutation(U)[:I] for _ in range(8)])
    idx2 = np.stack([np.random.permutation(T)[:I] for _ in range(8)])
    idx3 = np.stack([np.random.permutation(T)[:I] for _ in range(8)])
    idx4 = np.stack([np.random.permutation(T)[:I] for _ in range(8)])
    idx5 = np.stack([np.random.permutation(T)[:I] for _ in range(8)])
    idx6 = np.stack([np.random.permutation(U)[:I] for _ in range(8)])
    fd = mx_kscale(D)
    cachep = pack_weight(n((D, T)) / fd[:, None], "e4m3")
    draftp = pack_weight(n((D, U)) / fd[:, None], "e2m1")
    return {
        "query": (n((D, Q)) * 1.0 / np.sqrt(D) * fd[:, None]).astype(np.float32),
        "cache_words": cachep[0],
        "cache_scales": cachep[1],
        "draft_words": draftp[0],
        "draft_scales": draftp[1],
        "lam": (sgn((Q, 1))).astype(np.float32),
        "offs": striped8(idx),
        "offs2": striped8(idx2),
        "offs3": striped8(idx3),
        "offs4": striped8(idx4),
        "offs5": striped8(idx5),
        "offs6": striped8(idx6),
    }


def reference(query, cache_words, cache_scales, draft_words, draft_scales, lam, offs, offs2, offs3, offs4, offs5, offs6):
    idx = unstriped8(offs)
    idx2 = unstriped8(offs2)
    idx3 = unstriped8(offs3)
    idx4 = unstriped8(offs4)
    idx5 = unstriped8(offs5)
    idx6 = unstriped8(offs6)
    cacheu = unpack_weight(cache_words, cache_scales, "e4m3")
    draftu = unpack_weight(draft_words, draft_scales, "e2m1")
    queryq = mxq(f64(query), 0, "e4m3")
    a = queryq.T @ cacheu
    b = queryq.T @ draftu
    al = a * f64(lam)
    f1 = np.zeros((Q, T))
    f1[np.arange(Q)[:, None], idx2[np.arange(Q) % 128 // 16]] = pick8(b, idx, 16)
    c1 = al + f1
    f2 = np.zeros((Q, T))
    f2[np.arange(Q)[:, None], idx4[np.arange(Q) % 128 // 16]] = pick8(c1, idx3, 16)
    c2 = c1 * f64(lam) - f2
    y = pick8(c2, idx5, 16) + pick8(b, idx6, 16)
    return y

@@ -1,0 +1,125 @@
+from contextlib import ExitStack
+
+import concourse.mybir as mybir
+
+D, T, U, I, Q = 512, 1024, 1024, 512, 128
+FLOPS = 2 * D * Q * (T + U)
+
+F32 = mybir.dt.float32
+BF16 = mybir.dt.bfloat16
+I32 = mybir.dt.int32
+U32 = mybir.dt.uint32
+U16 = mybir.dt.uint16
+U8 = mybir.dt.uint8
+FP8X4 = mybir.dt.float8_e4m3fn_x4
+FP4X4 = mybir.dt.float4_e2m1fn_x4
+MULT = mybir.AluOpType.mult
+ADD = mybir.AluOpType.add
+SUB = mybir.AluOpType.subtract
+COPY = mybir.ActivationFunctionType.Copy
+
+P = 128
+PACK = 4
+BANK = 512
+HALF = I // 2
+PER_COL = 16
+
+
+def tile_attend_agedpage_two_kernel(tc, query, cache_words, cache_scales, draft_words, draft_scales, lam,
+                                     offs, offs2, offs3, offs4, offs5, offs6, out):
+    nc = tc.nc
+    with ExitStack() as ctx:
+        sb = ctx.enter_context(tc.tile_pool(name="sb", bufs=1))
+        ps = ctx.enter_context(tc.psum_pool(name="ps", bufs=1))
+
+        def load_list(src, name):
+            lst = sb.tile([P, I // PER_COL], U16, name=name)
+            nc.sync.dma_start(lst[:], src)
+            return lst
+
+        def half_of(lst, h):
+            cols = HALF // PER_COL
+            return lst[:, h * cols:(h + 1) * cols]
+
+        def load_scales(engine, plane, src):
+            for quad in range(4):
+                engine.dma_start(plane[32 * quad:32 * quad + 4, :].bitcast(I32),
+                                 src[0, 4 * quad:4 * quad + 4, :].bitcast(I32))
+
+        d_scale = sb.tile([P, U], U8, align_bytes=64)
+        c_scale = sb.tile([P, T], U8, align_bytes=64)
+        nc.vector.memset(d_scale[:].bitcast(I32), 0)
+        nc.vector.memset(c_scale[:].bitcast(I32), 0)
+
+        q_raw = sb.tile([P, PACK, Q], F32)
+        nc.sync.dma_start(q_raw[:], query.rearrange("(p j) q -> p j q", j=PACK))
+        load_scales(nc.scalar, d_scale, draft_scales)
+        d_words = sb.tile([P, 2 * U], U8, align_bytes=64)
+        nc.sync.dma_start(d_words[:].bitcast(I32), draft_words[0].bitcast(I32))
+        l1 = load_list(offs, "l1")
+        l2 = load_list(offs2, "l2")
+        c_words = sb.tile([P, T], U32, align_bytes=64)
+        nc.sync.dma_start(c_words[:].bitcast(I32), cache_words[0].rearrange("p n t -> p (n t)").bitcast(I32))
+        load_scales(nc.sync, c_scale, cache_scales)
+        lam_sb = sb.tile([P, 1], F32)
+        nc.sync.dma_start(lam_sb[:], lam)
+        l6 = load_list(offs6, "l6")
+        l3 = load_list(offs3, "l3")
+        l4 = load_list(offs4, "l4")
+        l5 = load_list(offs5, "l5")
+
+        f1 = sb.tile([P, T], F32)
+        f2 = sb.tile([P, T], F32)
+        nc.vector.memset(f1[:], 0.0)
+        nc.vector.memset(f2[:], 0.0)
+
+        q_bf = sb.tile([P, Q, PACK], BF16, align_bytes=64)
+        nc.vector.tensor_copy(out=q_bf[:], in_=q_raw[:].rearrange("p j q -> p q j"))
+        q_codes = sb.tile([P, Q], U32, align_bytes=64)
+        q_scale = sb.tile([P, Q], U8, align_bytes=64)
+        nc.vector.quantize_mx(out=q_codes[:].bitcast(FP8X4), scales=q_scale[:],
+                              in_=q_bf[:].rearrange("p q j -> p (q j)"))
+
+        b = sb.tile([P, U], F32)
+        for k in range(U // BANK):
+            cols = slice(k * BANK, (k + 1) * BANK)
+            b_ps = ps.tile([P, BANK], F32, name="b_ps%d" % k)
+            nc.tensor.matmul_mx(out=b_ps[:], lhsT=q_codes[:].bitcast(FP8X4), lhsT_scale=q_scale[:],
+                                rhs=d_words[:, 2 * k * BANK:2 * (k + 1) * BANK].bitcast(FP4X4),
+                                rhs_scale=d_scale[:, cols], start=True, stop=True)
+            if k == 0:
+                nc.scalar.copy(out=b[:, cols], in_=b_ps[:])
+            else:
+                nc.vector.tensor_copy(out=b[:, cols], in_=b_ps[:])
+
+        def move(window, gather_list, target, scatter_list, name):
+            for h in range(2):
+                picked = sb.tile([P, HALF], F32, name="%s%d" % (name, h))
+                nc.vector.tensor_copy(picked[:], window[:].indirect(half_of(gather_list, h)))
+                nc.scalar.activation(target[:].indirect(half_of(scatter_list, h)), picked[:], COPY)
+
+        move(b, l1, f1, l2, "g1")
+
+        b6 = sb.tile([P, I], F32)
+        nc.vector.tensor_copy(b6[:], b[:].indirect(l6[:]))
+
+        c1 = sb.tile([P, T], F32)
+        for k in range(T // BANK):
+            cols = slice(k * BANK, (k + 1) * BANK)
+            a_ps = ps.tile([P, BANK], F32, name="a_ps%d" % k)
+            nc.tensor.matmul_mx(out=a_ps[:], lhsT=q_codes[:].bitcast(FP8X4), lhsT_scale=q_scale[:],
+                                rhs=c_words[:, cols].bitcast(FP8X4), rhs_scale=c_scale[:, cols],
+                                start=True, stop=True)
+            nc.vector.scalar_tensor_tensor(out=c1[:, cols], in0=a_ps[:], scalar=lam_sb[:], in1=f1[:, cols],
+                                           op0=MULT, op1=ADD)
+
+        move(c1, l3, f2, l4, "g3")
+
+        c2 = sb.tile([P, T], F32)
+        nc.vector.scalar_tensor_tensor(out=c2[:], in0=c1[:], scalar=lam_sb[:], in1=f2[:], op0=MULT, op1=SUB)
+
+        for h in range(2):
+            cols = slice(h * HALF, (h + 1) * HALF)
+            res = sb.tile([P, HALF], F32, name="res%d" % h)
+            nc.vector.tensor_tensor(res[:], c2[:].indirect(half_of(l5, h)), b6[:, cols], ADD)
+            (nc.sync if h == 0 else nc.scalar).dma_start(out[:, cols], res[:])

@@ -23,6 +23,9 @@ PACK = 4
 BANK = 512
 HALF = I // 2
 PER_COL = 16
+Q_SPLIT = 88
+C_SPLIT = 224
+B_WIDTHS = (256, 256, 256, 128, 128)
 
 
 def tile_attend_agedpage_two_kernel(tc, query, cache_words, cache_scales, draft_words, draft_scales, lam,
@@ -53,17 +56,17 @@ def tile_attend_agedpage_two_kernel(tc, query, cache_words, cache_scales, draft_
 
         q_raw = sb.tile([P, PACK, Q], F32)
         nc.sync.dma_start(q_raw[:], query.rearrange("(p j) q -> p j q", j=PACK))
-        load_scales(nc.scalar, d_scale, draft_scales)
         d_words = sb.tile([P, 2 * U], U8, align_bytes=64)
         nc.sync.dma_start(d_words[:].bitcast(I32), draft_words[0].bitcast(I32))
+        load_scales(nc.sync, d_scale, draft_scales)
         l1 = load_list(offs, "l1")
         l2 = load_list(offs2, "l2")
+        l6 = load_list(offs6, "l6")
         c_words = sb.tile([P, T], U32, align_bytes=64)
         nc.sync.dma_start(c_words[:].bitcast(I32), cache_words[0].rearrange("p n t -> p (n t)").bitcast(I32))
         load_scales(nc.sync, c_scale, cache_scales)
         lam_sb = sb.tile([P, 1], F32)
         nc.sync.dma_start(lam_sb[:], lam)
-        l6 = load_list(offs6, "l6")
         l3 = load_list(offs3, "l3")
         l4 = load_list(offs4, "l4")
         l5 = load_list(offs5, "l5")
@@ -71,55 +74,68 @@ def tile_attend_agedpage_two_kernel(tc, query, cache_words, cache_scales, draft_
         f1 = sb.tile([P, T], F32)
         f2 = sb.tile([P, T], F32)
         nc.vector.memset(f1[:], 0.0)
-        nc.vector.memset(f2[:], 0.0)
+        nc.gpsimd.memset(f2[:], 0.0)
 
         q_bf = sb.tile([P, Q, PACK], BF16, align_bytes=64)
-        nc.vector.tensor_copy(out=q_bf[:], in_=q_raw[:].rearrange("p j q -> p q j"))
+        nc.vector.tensor_copy(out=q_bf[:, :Q_SPLIT, :], in_=q_raw[:, :, :Q_SPLIT].rearrange("p j q -> p q j"))
+        nc.scalar.copy(out=q_bf[:, Q_SPLIT:, :], in_=q_raw[:, :, Q_SPLIT:].rearrange("p j q -> p q j"))
         q_codes = sb.tile([P, Q], U32, align_bytes=64)
         q_scale = sb.tile([P, Q], U8, align_bytes=64)
         nc.vector.quantize_mx(out=q_codes[:].bitcast(FP8X4), scales=q_scale[:],
                               in_=q_bf[:].rearrange("p q j -> p (q j)"))
 
-        b = sb.tile([P, U], F32)
-        for k in range(U // BANK):
-            cols = slice(k * BANK, (k + 1) * BANK)
-            b_ps = ps.tile([P, BANK], F32, name="b_ps%d" % k)
+        b = sb.tile([P, U], F32, tag="scores")
+        first = 0
+        for k, width in enumerate(B_WIDTHS):
+            cols = slice(first, first + width)
+            b_ps = ps.tile([P, width], F32, name="b_ps%d" % k)
             nc.tensor.matmul_mx(out=b_ps[:], lhsT=q_codes[:].bitcast(FP8X4), lhsT_scale=q_scale[:],
-                                rhs=d_words[:, 2 * k * BANK:2 * (k + 1) * BANK].bitcast(FP4X4),
+                                rhs=d_words[:, 2 * first:2 * (first + width)].bitcast(FP4X4),
                                 rhs_scale=d_scale[:, cols], start=True, stop=True)
-            if k == 0:
+            if k % 2 == 1:
                 nc.scalar.copy(out=b[:, cols], in_=b_ps[:])
             else:
                 nc.vector.tensor_copy(out=b[:, cols], in_=b_ps[:])
+            first = first + width
 
         def move(window, gather_list, target, scatter_list, name):
-            for h in range(2):
-                picked = sb.tile([P, HALF], F32, name="%s%d" % (name, h))
-                nc.vector.tensor_copy(picked[:], window[:].indirect(half_of(gather_list, h)))
-                nc.scalar.activation(target[:].indirect(half_of(scatter_list, h)), picked[:], COPY)
+            picked = sb.tile([P, I], F32, name=name)
+            nc.vector.tensor_copy(picked[:, :HALF], window[:].indirect(half_of(gather_list, 0)))
+            nc.scalar.activation(picked[:, HALF:], window[:].indirect(half_of(gather_list, 1)), COPY)
+            nc.scalar.activation(target[:].indirect(scatter_list[:]), picked[:], COPY)
 
         move(b, l1, f1, l2, "g1")
 
         b6 = sb.tile([P, I], F32)
         nc.vector.tensor_copy(b6[:], b[:].indirect(l6[:]))
 
-        c1 = sb.tile([P, T], F32)
+        c1 = sb.tile([P, T], F32, tag="scores")
+        a_banks = []
         for k in range(T // BANK):
             cols = slice(k * BANK, (k + 1) * BANK)
             a_ps = ps.tile([P, BANK], F32, name="a_ps%d" % k)
             nc.tensor.matmul_mx(out=a_ps[:], lhsT=q_codes[:].bitcast(FP8X4), lhsT_scale=q_scale[:],
                                 rhs=c_words[:, cols].bitcast(FP8X4), rhs_scale=c_scale[:, cols],
                                 start=True, stop=True)
-            nc.vector.scalar_tensor_tensor(out=c1[:, cols], in0=a_ps[:], scalar=lam_sb[:], in1=f1[:, cols],
-                                           op0=MULT, op1=ADD)
+            a_banks.append(a_ps)
+        al_head = sb.tile([P, C_SPLIT], F32)
+        nc.vector.tensor_scalar(al_head[:], a_banks[0][:, :C_SPLIT], lam_sb[:], None, MULT)
+        nc.gpsimd.tensor_tensor(c1[:, :C_SPLIT], al_head[:], f1[:, :C_SPLIT], ADD)
+        nc.vector.scalar_tensor_tensor(out=c1[:, C_SPLIT:BANK], in0=a_banks[0][:, C_SPLIT:], scalar=lam_sb[:],
+                                       in1=f1[:, C_SPLIT:BANK], op0=MULT, op1=ADD)
+        nc.vector.scalar_tensor_tensor(out=c1[:, BANK:], in0=a_banks[1][:], scalar=lam_sb[:], in1=f1[:, BANK:],
+                                       op0=MULT, op1=ADD)
 
         move(c1, l3, f2, l4, "g3")
 
         c2 = sb.tile([P, T], F32)
         nc.vector.scalar_tensor_tensor(out=c2[:], in0=c1[:], scalar=lam_sb[:], in1=f2[:], op0=MULT, op1=SUB)
 
-        for h in range(2):
-            cols = slice(h * HALF, (h + 1) * HALF)
-            res = sb.tile([P, HALF], F32, name="res%d" % h)
-            nc.vector.tensor_tensor(res[:], c2[:].indirect(half_of(l5, h)), b6[:, cols], ADD)
-            (nc.sync if h == 0 else nc.scalar).dma_start(out[:, cols], res[:])
+        res0 = sb.tile([P, HALF], F32)
+        nc.vector.tensor_tensor(res0[:], c2[:].indirect(half_of(l5, 0)), b6[:, :HALF], ADD)
+        g5 = sb.tile([P, HALF], F32)
+        nc.scalar.activation(g5[:], c2[:].indirect(half_of(l5, 1)), COPY)
+        nc.scalar.dma_start(out[:, :HALF], res0[:])
+        res1 = sb.tile([P, HALF], F32)
+        nc.vector.tensor_tensor(res1[:], g5[:], b6[:, HALF:], ADD)
+        nc.sync.dma_start(out[:, HALF:], res1[:])

@@ -23,7 +23,7 @@ PACK = 4
 BANK = 512
 HALF = I // 2
 PER_COL = 16
-Q_SPLIT = 88
+Q_SPLIT = 64
 C_SPLIT = 224
 B_WIDTHS = (256, 256, 256, 128, 128)
 
@@ -45,9 +45,8 @@ def tile_attend_agedpage_two_kernel(tc, query, cache_words, cache_scales, draft_
             return lst[:, h * cols:(h + 1) * cols]
 
         def load_scales(engine, plane, src):
-            for quad in range(4):
-                engine.dma_start(plane[32 * quad:32 * quad + 4, :].bitcast(I32),
-                                 src[0, 4 * quad:4 * quad + 4, :].bitcast(I32))
+            for r in range(4):
+                engine.dma_start(plane[r:P:32, :].bitcast(I32), src[0, r:16:4, :].bitcast(I32))
 
         d_scale = sb.tile([P, U], U8, align_bytes=64)
         c_scale = sb.tile([P, T], U8, align_bytes=64)
@@ -56,9 +55,12 @@ def tile_attend_agedpage_two_kernel(tc, query, cache_words, cache_scales, draft_
 
         q_raw = sb.tile([P, PACK, Q], F32)
         nc.sync.dma_start(q_raw[:], query.rearrange("(p j) q -> p j q", j=PACK))
-        d_words = sb.tile([P, 2 * U], U8, align_bytes=64)
-        nc.sync.dma_start(d_words[:].bitcast(I32), draft_words[0].bitcast(I32))
         load_scales(nc.sync, d_scale, draft_scales)
+        d_words = []
+        for h in range(2):
+            words = sb.tile([P, U], U8, align_bytes=64, name="d_words%d" % h)
+            nc.sync.dma_start(words[:].bitcast(I32), draft_words[0, :, h * U:(h + 1) * U].bitcast(I32))
+            d_words.append(words)
         l1 = load_list(offs, "l1")
         l2 = load_list(offs2, "l2")
         l6 = load_list(offs6, "l6")
@@ -74,7 +76,7 @@ def tile_attend_agedpage_two_kernel(tc, query, cache_words, cache_scales, draft_
         f1 = sb.tile([P, T], F32)
         f2 = sb.tile([P, T], F32)
         nc.vector.memset(f1[:], 0.0)
-        nc.gpsimd.memset(f2[:], 0.0)
+        nc.vector.memset(f2[:], 0.0)
 
         q_bf = sb.tile([P, Q, PACK], BF16, align_bytes=64)
         nc.vector.tensor_copy(out=q_bf[:, :Q_SPLIT, :], in_=q_raw[:, :, :Q_SPLIT].rearrange("p j q -> p q j"))
@@ -90,7 +92,7 @@ def tile_attend_agedpage_two_kernel(tc, query, cache_words, cache_scales, draft_
             cols = slice(first, first + width)
             b_ps = ps.tile([P, width], F32, name="b_ps%d" % k)
             nc.tensor.matmul_mx(out=b_ps[:], lhsT=q_codes[:].bitcast(FP8X4), lhsT_scale=q_scale[:],
-                                rhs=d_words[:, 2 * first:2 * (first + width)].bitcast(FP4X4),
+                                rhs=d_words[first // BANK][:, 2 * (first % BANK):2 * (first % BANK + width)].bitcast(FP4X4),
                                 rhs_scale=d_scale[:, cols], start=True, stop=True)
             if k % 2 == 1:
                 nc.scalar.copy(out=b[:, cols], in_=b_ps[:])

@@ -1,6 +1,7 @@
 from contextlib import ExitStack
 
 import concourse.mybir as mybir
+from concourse.masks import make_identity
 
 D, T, U, I, Q = 512, 1024, 1024, 512, 128
 FLOPS = 2 * D * Q * (T + U)
@@ -21,11 +22,15 @@ COPY = mybir.ActivationFunctionType.Copy
 P = 128
 PACK = 4
 BANK = 512
+QUADRANT = 32
+SCALE_ROWS = D // 32
+ENTRIES_PER_COLUMN = 16
 HALF = I // 2
-PER_COL = 16
-Q_SPLIT = 64
-C_SPLIT = 224
+
+CAST_ON_VECTOR = 64
 B_WIDTHS = (256, 256, 256, 128, 128)
+GPSIMD_COLUMNS = 304
+PARKED_FROM = GPSIMD_COLUMNS // P * P
 
 
 def tile_attend_agedpage_two_kernel(tc, query, cache_words, cache_scales, draft_words, draft_scales, lam,
@@ -36,51 +41,50 @@ def tile_attend_agedpage_two_kernel(tc, query, cache_words, cache_scales, draft_
         ps = ctx.enter_context(tc.psum_pool(name="ps", bufs=1))
 
         def load_list(src, name):
-            lst = sb.tile([P, I // PER_COL], U16, name=name)
+            lst = sb.tile([P, I // ENTRIES_PER_COLUMN], U16, name=name)
             nc.sync.dma_start(lst[:], src)
             return lst
 
         def half_of(lst, h):
-            cols = HALF // PER_COL
+            cols = HALF // ENTRIES_PER_COLUMN
             return lst[:, h * cols:(h + 1) * cols]
 
-        def load_scales(engine, plane, src):
+        def load_scales(scale_tile, src):
             for r in range(4):
-                engine.dma_start(plane[r:P:32, :].bitcast(I32), src[0, r:16:4, :].bitcast(I32))
+                nc.sync.dma_start(scale_tile[r:P:QUADRANT, :].bitcast(I32), src[0, r:SCALE_ROWS:4, :].bitcast(I32))
 
         d_scale = sb.tile([P, U], U8, align_bytes=64)
-        c_scale = sb.tile([P, T], U8, align_bytes=64)
+        c_scale = sb.tile([P, T], U8, align_bytes=64, tag="c_scale")
         nc.vector.memset(d_scale[:].bitcast(I32), 0)
         nc.vector.memset(c_scale[:].bitcast(I32), 0)
 
         q_raw = sb.tile([P, PACK, Q], F32)
         nc.sync.dma_start(q_raw[:], query.rearrange("(p j) q -> p j q", j=PACK))
-        load_scales(nc.sync, d_scale, draft_scales)
+        load_scales(d_scale, draft_scales)
         d_words = []
-        for h in range(2):
-            words = sb.tile([P, U], U8, align_bytes=64, name="d_words%d" % h)
-            nc.sync.dma_start(words[:].bitcast(I32), draft_words[0, :, h * U:(h + 1) * U].bitcast(I32))
+        for h in range(U // BANK):
+            words = sb.tile([P, 2 * BANK], U8, align_bytes=64, name="d_words%d" % h)
+            nc.sync.dma_start(words[:].bitcast(I32), draft_words[0, :, 2 * h * BANK:2 * (h + 1) * BANK].bitcast(I32))
             d_words.append(words)
-        l1 = load_list(offs, "l1")
-        l2 = load_list(offs2, "l2")
-        l6 = load_list(offs6, "l6")
-        c_words = sb.tile([P, T], U32, align_bytes=64)
+        idx = load_list(offs, "idx")
+        idx2 = load_list(offs2, "idx2")
+        c_words = sb.tile([P, T], U32, align_bytes=64, tag="c_words")
         nc.sync.dma_start(c_words[:].bitcast(I32), cache_words[0].rearrange("p n t -> p (n t)").bitcast(I32))
-        load_scales(nc.sync, c_scale, cache_scales)
+        load_scales(c_scale, cache_scales)
         lam_sb = sb.tile([P, 1], F32)
         nc.sync.dma_start(lam_sb[:], lam)
-        l3 = load_list(offs3, "l3")
-        l4 = load_list(offs4, "l4")
-        l5 = load_list(offs5, "l5")
+        idx6 = load_list(offs6, "idx6")
+        idx3 = load_list(offs3, "idx3")
+        idx4 = load_list(offs4, "idx4")
+        idx5 = load_list(offs5, "idx5")
 
         f1 = sb.tile([P, T], F32)
-        f2 = sb.tile([P, T], F32)
         nc.vector.memset(f1[:], 0.0)
-        nc.vector.memset(f2[:], 0.0)
 
         q_bf = sb.tile([P, Q, PACK], BF16, align_bytes=64)
-        nc.vector.tensor_copy(out=q_bf[:, :Q_SPLIT, :], in_=q_raw[:, :, :Q_SPLIT].rearrange("p j q -> p q j"))
-        nc.scalar.copy(out=q_bf[:, Q_SPLIT:, :], in_=q_raw[:, :, Q_SPLIT:].rearrange("p j q -> p q j"))
+        nc.vector.tensor_copy(out=q_bf[:, :CAST_ON_VECTOR, :],
+                              in_=q_raw[:, :, :CAST_ON_VECTOR].rearrange("p j q -> p q j"))
+        nc.scalar.copy(out=q_bf[:, CAST_ON_VECTOR:, :], in_=q_raw[:, :, CAST_ON_VECTOR:].rearrange("p j q -> p q j"))
         q_codes = sb.tile([P, Q], U32, align_bytes=64)
         q_scale = sb.tile([P, Q], U8, align_bytes=64)
         nc.vector.quantize_mx(out=q_codes[:].bitcast(FP8X4), scales=q_scale[:],
@@ -90,9 +94,10 @@ def tile_attend_agedpage_two_kernel(tc, query, cache_words, cache_scales, draft_
         first = 0
         for k, width in enumerate(B_WIDTHS):
             cols = slice(first, first + width)
-            b_ps = ps.tile([P, width], F32, name="b_ps%d" % k)
+            in_half = first % BANK
+            b_ps = ps.tile([P, width], F32, name="b_ps%d" % k, tag="bank%d" % k)
             nc.tensor.matmul_mx(out=b_ps[:], lhsT=q_codes[:].bitcast(FP8X4), lhsT_scale=q_scale[:],
-                                rhs=d_words[first // BANK][:, 2 * (first % BANK):2 * (first % BANK + width)].bitcast(FP4X4),
+                                rhs=d_words[first // BANK][:, 2 * in_half:2 * (in_half + width)].bitcast(FP4X4),
                                 rhs_scale=d_scale[:, cols], start=True, stop=True)
             if k % 2 == 1:
                 nc.scalar.copy(out=b[:, cols], in_=b_ps[:])
@@ -106,12 +111,11 @@ def tile_attend_agedpage_two_kernel(tc, query, cache_words, cache_scales, draft_
             nc.scalar.activation(picked[:, HALF:], window[:].indirect(half_of(gather_list, 1)), COPY)
             nc.scalar.activation(target[:].indirect(scatter_list[:]), picked[:], COPY)
 
-        move(b, l1, f1, l2, "g1")
+        move(b, idx, f1, idx2, "b_picked")
 
         b6 = sb.tile([P, I], F32)
-        nc.vector.tensor_copy(b6[:], b[:].indirect(l6[:]))
+        nc.vector.tensor_copy(b6[:], b[:].indirect(idx6[:]))
 
-        c1 = sb.tile([P, T], F32, tag="scores")
         a_banks = []
         for k in range(T // BANK):
             cols = slice(k * BANK, (k + 1) * BANK)
@@ -120,24 +124,52 @@ def tile_attend_agedpage_two_kernel(tc, query, cache_words, cache_scales, draft_
                                 rhs=c_words[:, cols].bitcast(FP8X4), rhs_scale=c_scale[:, cols],
                                 start=True, stop=True)
             a_banks.append(a_ps)
-        al_head = sb.tile([P, C_SPLIT], F32)
-        nc.vector.tensor_scalar(al_head[:], a_banks[0][:, :C_SPLIT], lam_sb[:], None, MULT)
-        nc.gpsimd.tensor_tensor(c1[:, :C_SPLIT], al_head[:], f1[:, :C_SPLIT], ADD)
-        nc.vector.scalar_tensor_tensor(out=c1[:, C_SPLIT:BANK], in0=a_banks[0][:, C_SPLIT:], scalar=lam_sb[:],
-                                       in1=f1[:, C_SPLIT:BANK], op0=MULT, op1=ADD)
+
+        f2 = sb.tile([P, T], F32, align_bytes=64, tag="c_words")
+        nc.gpsimd.memset(f2[:], 0.0)
+        ident = sb.tile([P, P], F32, align_bytes=64, tag="c_scale")
+        make_identity(nc, ident[:])
+
+        c1 = sb.tile([P, T], F32, tag="scores")
+        a_lam = sb.tile([P, GPSIMD_COLUMNS], F32)
+        nc.vector.tensor_scalar(a_lam[:], a_banks[0][:, :GPSIMD_COLUMNS], lam_sb[:], None, MULT)
+        nc.gpsimd.tensor_tensor(c1[:, :GPSIMD_COLUMNS], a_lam[:], f1[:, :GPSIMD_COLUMNS], ADD)
+        nc.vector.scalar_tensor_tensor(out=c1[:, GPSIMD_COLUMNS:BANK], in0=a_banks[0][:, GPSIMD_COLUMNS:],
+                                       scalar=lam_sb[:], in1=f1[:, GPSIMD_COLUMNS:BANK], op0=MULT, op1=ADD)
         nc.vector.scalar_tensor_tensor(out=c1[:, BANK:], in0=a_banks[1][:], scalar=lam_sb[:], in1=f1[:, BANK:],
                                        op0=MULT, op1=ADD)
 
-        move(c1, l3, f2, l4, "g3")
+        move(c1, idx3, f2, idx4, "c1_picked")
 
+        c1_lam = sb.tile([P, GPSIMD_COLUMNS], F32)
+        nc.vector.tensor_scalar(c1_lam[:], c1[:, :GPSIMD_COLUMNS], lam_sb[:], None, MULT)
+        spans = ((PARKED_FROM, BANK), (BANK, T))
+        c1_turned = []
+        for k, (lo, hi) in enumerate(spans):
+            turned_ps = ps.tile([P, hi - lo], F32, name="turned_ps%d" % k, tag="bank%d" % k)
+            for col in range(0, hi - lo, P):
+                nc.tensor.transpose(turned_ps[:, col:col + P], c1[:, lo + col:lo + col + P], ident[:])
+            turned = sb.tile([P, hi - lo], F32, name="turned%d" % k)
+            nc.vector.tensor_copy(out=turned[:], in_=turned_ps[:])
+            c1_turned.append(turned)
+        c1_banks = []
+        for k, (lo, hi) in enumerate(spans):
+            c1_ps = ps.tile([P, hi - lo], F32, name="c1_ps%d" % k, tag="bank%d" % (len(spans) + k))
+            for col in range(0, hi - lo, P):
+                nc.tensor.transpose(c1_ps[:, col:col + P], c1_turned[k][:, col:col + P], ident[:])
+            c1_banks.append(c1_ps)
         c2 = sb.tile([P, T], F32)
-        nc.vector.scalar_tensor_tensor(out=c2[:], in0=c1[:], scalar=lam_sb[:], in1=f2[:], op0=MULT, op1=SUB)
+        nc.gpsimd.tensor_tensor(c2[:, :GPSIMD_COLUMNS], c1_lam[:], f2[:, :GPSIMD_COLUMNS], SUB)
+        nc.vector.scalar_tensor_tensor(out=c2[:, GPSIMD_COLUMNS:BANK], in0=c1_banks[0][:, GPSIMD_COLUMNS - PARKED_FROM:],
+                                       scalar=lam_sb[:], in1=f2[:, GPSIMD_COLUMNS:BANK], op0=MULT, op1=SUB)
+        nc.vector.scalar_tensor_tensor(out=c2[:, BANK:], in0=c1_banks[1][:], scalar=lam_sb[:], in1=f2[:, BANK:],
+                                       op0=MULT, op1=SUB)
 
-        res0 = sb.tile([P, HALF], F32)
-        nc.vector.tensor_tensor(res0[:], c2[:].indirect(half_of(l5, 0)), b6[:, :HALF], ADD)
-        g5 = sb.tile([P, HALF], F32)
-        nc.scalar.activation(g5[:], c2[:].indirect(half_of(l5, 1)), COPY)
-        nc.scalar.dma_start(out[:, :HALF], res0[:])
-        res1 = sb.tile([P, HALF], F32)
-        nc.vector.tensor_tensor(res1[:], g5[:], b6[:, HALF:], ADD)
-        nc.sync.dma_start(out[:, HALF:], res1[:])
+        out_first = sb.tile([P, HALF], F32)
+        nc.vector.tensor_tensor(out_first[:], c2[:].indirect(half_of(idx5, 0)), b6[:, :HALF], ADD)
+        c2_picked = sb.tile([P, HALF], F32)
+        nc.scalar.activation(c2_picked[:], c2[:].indirect(half_of(idx5, 1)), COPY)
+        nc.scalar.dma_start(out[:, :HALF], out_first[:])
+        out_second = sb.tile([P, HALF], F32)
+        nc.vector.tensor_tensor(out_second[:], c2_picked[:], b6[:, HALF:], ADD)
+        nc.sync.dma_start(out[:, HALF:], out_second[:])

from contextlib import ExitStack

import concourse.mybir as mybir
from concourse.masks import make_identity

D, T, U, I, Q = 512, 1024, 1024, 512, 128
FLOPS = 2 * D * Q * (T + U)

F32 = mybir.dt.float32
BF16 = mybir.dt.bfloat16
I32 = mybir.dt.int32
U32 = mybir.dt.uint32
U16 = mybir.dt.uint16
U8 = mybir.dt.uint8
FP8X4 = mybir.dt.float8_e4m3fn_x4
FP4X4 = mybir.dt.float4_e2m1fn_x4
MULT = mybir.AluOpType.mult
ADD = mybir.AluOpType.add
SUB = mybir.AluOpType.subtract
COPY = mybir.ActivationFunctionType.Copy

P = 128
PACK = 4
BANK = 512
QUADRANT = 32
SCALE_ROWS = D // 32
ENTRIES_PER_COLUMN = 16
HALF = I // 2

CAST_ON_VECTOR = 64
B_WIDTHS = (256, 256, 256, 128, 128)
GPSIMD_COLUMNS = 304
PARKED_FROM = GPSIMD_COLUMNS // P * P


def tile_attend_agedpage_two_kernel(tc, query, cache_words, cache_scales, draft_words, draft_scales, lam,
                                     offs, offs2, offs3, offs4, offs5, offs6, out):
    nc = tc.nc
    with ExitStack() as ctx:
        sb = ctx.enter_context(tc.tile_pool(name="sb", bufs=1))
        ps = ctx.enter_context(tc.psum_pool(name="ps", bufs=1))

        def load_list(src, name):
            lst = sb.tile([P, I // ENTRIES_PER_COLUMN], U16, name=name)
            nc.sync.dma_start(lst[:], src)
            return lst

        def half_of(lst, h):
            cols = HALF // ENTRIES_PER_COLUMN
            return lst[:, h * cols:(h + 1) * cols]

        def load_scales(scale_tile, src):
            for r in range(4):
                nc.sync.dma_start(scale_tile[r:P:QUADRANT, :].bitcast(I32), src[0, r:SCALE_ROWS:4, :].bitcast(I32))

        d_scale = sb.tile([P, U], U8, align_bytes=64)
        c_scale = sb.tile([P, T], U8, align_bytes=64, tag="c_scale")
        nc.vector.memset(d_scale[:].bitcast(I32), 0)
        nc.vector.memset(c_scale[:].bitcast(I32), 0)

        q_raw = sb.tile([P, PACK, Q], F32)
        nc.sync.dma_start(q_raw[:], query.rearrange("(p j) q -> p j q", j=PACK))
        load_scales(d_scale, draft_scales)
        d_words = []
        for h in range(U // BANK):
            words = sb.tile([P, 2 * BANK], U8, align_bytes=64, name="d_words%d" % h)
            nc.sync.dma_start(words[:].bitcast(I32), draft_words[0, :, 2 * h * BANK:2 * (h + 1) * BANK].bitcast(I32))
            d_words.append(words)
        idx = load_list(offs, "idx")
        idx2 = load_list(offs2, "idx2")
        c_words = sb.tile([P, T], U32, align_bytes=64, tag="c_words")
        nc.sync.dma_start(c_words[:].bitcast(I32), cache_words[0].rearrange("p n t -> p (n t)").bitcast(I32))
        load_scales(c_scale, cache_scales)
        lam_sb = sb.tile([P, 1], F32)
        nc.sync.dma_start(lam_sb[:], lam)
        idx6 = load_list(offs6, "idx6")
        idx3 = load_list(offs3, "idx3")
        idx4 = load_list(offs4, "idx4")
        idx5 = load_list(offs5, "idx5")

        f1 = sb.tile([P, T], F32)
        nc.vector.memset(f1[:], 0.0)

        q_bf = sb.tile([P, Q, PACK], BF16, align_bytes=64)
        nc.vector.tensor_copy(out=q_bf[:, :CAST_ON_VECTOR, :],
                              in_=q_raw[:, :, :CAST_ON_VECTOR].rearrange("p j q -> p q j"))
        nc.scalar.copy(out=q_bf[:, CAST_ON_VECTOR:, :], in_=q_raw[:, :, CAST_ON_VECTOR:].rearrange("p j q -> p q j"))
        q_codes = sb.tile([P, Q], U32, align_bytes=64)
        q_scale = sb.tile([P, Q], U8, align_bytes=64)
        nc.vector.quantize_mx(out=q_codes[:].bitcast(FP8X4), scales=q_scale[:],
                              in_=q_bf[:].rearrange("p q j -> p (q j)"))

        b = sb.tile([P, U], F32, tag="scores")
        first = 0
        for k, width in enumerate(B_WIDTHS):
            cols = slice(first, first + width)
            in_half = first % BANK
            b_ps = ps.tile([P, width], F32, name="b_ps%d" % k, tag="bank%d" % k)
            nc.tensor.matmul_mx(out=b_ps[:], lhsT=q_codes[:].bitcast(FP8X4), lhsT_scale=q_scale[:],
                                rhs=d_words[first // BANK][:, 2 * in_half:2 * (in_half + width)].bitcast(FP4X4),
                                rhs_scale=d_scale[:, cols], start=True, stop=True)
            if k % 2 == 1:
                nc.scalar.copy(out=b[:, cols], in_=b_ps[:])
            else:
                nc.vector.tensor_copy(out=b[:, cols], in_=b_ps[:])
            first = first + width

        def move(window, gather_list, target, scatter_list, name):
            picked = sb.tile([P, I], F32, name=name)
            nc.vector.tensor_copy(picked[:, :HALF], window[:].indirect(half_of(gather_list, 0)))
            nc.scalar.activation(picked[:, HALF:], window[:].indirect(half_of(gather_list, 1)), COPY)
            nc.scalar.activation(target[:].indirect(scatter_list[:]), picked[:], COPY)

        move(b, idx, f1, idx2, "b_picked")

        b6 = sb.tile([P, I], F32)
        nc.vector.tensor_copy(b6[:], b[:].indirect(idx6[:]))

        a_banks = []
        for k in range(T // BANK):
            cols = slice(k * BANK, (k + 1) * BANK)
            a_ps = ps.tile([P, BANK], F32, name="a_ps%d" % k)
            nc.tensor.matmul_mx(out=a_ps[:], lhsT=q_codes[:].bitcast(FP8X4), lhsT_scale=q_scale[:],
                                rhs=c_words[:, cols].bitcast(FP8X4), rhs_scale=c_scale[:, cols],
                                start=True, stop=True)
            a_banks.append(a_ps)

        f2 = sb.tile([P, T], F32, align_bytes=64, tag="c_words")
        nc.gpsimd.memset(f2[:], 0.0)
        ident = sb.tile([P, P], F32, align_bytes=64, tag="c_scale")
        make_identity(nc, ident[:])

        c1 = sb.tile([P, T], F32, tag="scores")
        a_lam = sb.tile([P, GPSIMD_COLUMNS], F32)
        nc.vector.tensor_scalar(a_lam[:], a_banks[0][:, :GPSIMD_COLUMNS], lam_sb[:], None, MULT)
        nc.gpsimd.tensor_tensor(c1[:, :GPSIMD_COLUMNS], a_lam[:], f1[:, :GPSIMD_COLUMNS], ADD)
        nc.vector.scalar_tensor_tensor(out=c1[:, GPSIMD_COLUMNS:BANK], in0=a_banks[0][:, GPSIMD_COLUMNS:],
                                       scalar=lam_sb[:], in1=f1[:, GPSIMD_COLUMNS:BANK], op0=MULT, op1=ADD)
        nc.vector.scalar_tensor_tensor(out=c1[:, BANK:], in0=a_banks[1][:], scalar=lam_sb[:], in1=f1[:, BANK:],
                                       op0=MULT, op1=ADD)

        move(c1, idx3, f2, idx4, "c1_picked")

        c1_lam = sb.tile([P, GPSIMD_COLUMNS], F32)
        nc.vector.tensor_scalar(c1_lam[:], c1[:, :GPSIMD_COLUMNS], lam_sb[:], None, MULT)
        spans = ((PARKED_FROM, BANK), (BANK, T))
        c1_turned = []
        for k, (lo, hi) in enumerate(spans):
            turned_ps = ps.tile([P, hi - lo], F32, name="turned_ps%d" % k, tag="bank%d" % k)
            for col in range(0, hi - lo, P):
                nc.tensor.transpose(turned_ps[:, col:col + P], c1[:, lo + col:lo + col + P], ident[:])
            turned = sb.tile([P, hi - lo], F32, name="turned%d" % k)
            nc.vector.tensor_copy(out=turned[:], in_=turned_ps[:])
            c1_turned.append(turned)
        c1_banks = []
        for k, (lo, hi) in enumerate(spans):
            c1_ps = ps.tile([P, hi - lo], F32, name="c1_ps%d" % k, tag="bank%d" % (len(spans) + k))
            for col in range(0, hi - lo, P):
                nc.tensor.transpose(c1_ps[:, col:col + P], c1_turned[k][:, col:col + P], ident[:])
            c1_banks.append(c1_ps)
        c2 = sb.tile([P, T], F32)
        nc.gpsimd.tensor_tensor(c2[:, :GPSIMD_COLUMNS], c1_lam[:], f2[:, :GPSIMD_COLUMNS], SUB)
        nc.vector.scalar_tensor_tensor(out=c2[:, GPSIMD_COLUMNS:BANK], in0=c1_banks[0][:, GPSIMD_COLUMNS - PARKED_FROM:],
                                       scalar=lam_sb[:], in1=f2[:, GPSIMD_COLUMNS:BANK], op0=MULT, op1=SUB)
        nc.vector.scalar_tensor_tensor(out=c2[:, BANK:], in0=c1_banks[1][:], scalar=lam_sb[:], in1=f2[:, BANK:],
                                       op0=MULT, op1=SUB)

        out_first = sb.tile([P, HALF], F32)
        nc.vector.tensor_tensor(out_first[:], c2[:].indirect(half_of(idx5, 0)), b6[:, :HALF], ADD)
        c2_picked = sb.tile([P, HALF], F32)
        nc.scalar.activation(c2_picked[:], c2[:].indirect(half_of(idx5, 1)), COPY)
        nc.scalar.dma_start(out[:, :HALF], out_first[:])
        out_second = sb.tile([P, HALF], F32)
        nc.vector.tensor_tensor(out_second[:], c2_picked[:], b6[:, HALF:], ADD)
        nc.sync.dma_start(out[:, HALF:], out_second[:])
